import numpy as np
import ml_dtypes


def mxq(x, axis, fmt="e4m3"):
    dtype, down = {"e4m3": (ml_dtypes.float8_e4m3fn, 7), "e5m2": (ml_dtypes.float8_e5m2, 14)}[fmt]
    v = np.moveaxis(np.asarray(x, np.float32).astype(ml_dtypes.bfloat16).astype(np.float64), axis, -1)
    blocks = v.reshape(v.shape[:-1] + (-1, 32))
    amax = np.abs(blocks).max(-1, keepdims=True)
    byte = np.maximum(np.where(amax > 0, np.frexp(amax)[1] - 1 + 127, 0) - down, 1)
    scale = np.exp2(byte - 127.0)
    codes = (blocks / scale).astype(np.float32).astype(dtype).astype(np.float64)
    return np.moveaxis((codes * scale).reshape(v.shape), -1, axis)


WIDE = False


def mx_kscale(k):
    if not WIDE:
        return np.ones(k)
    levels = np.array([24, -24, 12, -12, 0])
    if k % 512:
        return np.exp2(np.random.permutation(np.resize(levels, k // 32))).repeat(32)
    a = np.empty((k // 512, 16))
    for p in range(k // 512):
        a[p, :8] = np.random.permutation(np.resize(levels, 8))
        for g in range(8):
            far = levels[np.abs(levels - a[p, g]) >= 10]
            a[p, g + 8] = far[np.random.randint(len(far))]
    return np.exp2(a.ravel()).repeat(32)


def f64(x):
    return np.asarray(x).astype(np.float64)


def striped(idx):
    return np.tile(idx.reshape(-1, 16).T, (8, 1)).astype(np.uint16)


def unstriped(offs):
    return offs[:16].T.reshape(-1).astype(np.int64)


E2M1 = np.array([0.0, 0.5, 1.0, 1.5, 2.0, 3.0, 4.0, 6.0, -0.0, -0.5, -1.0, -1.5, -2.0, -3.0, -4.0, -6.0])


def pack_weight(w, fmt):
    k, n = w.shape
    w = f64(np.asarray(w, np.float32).astype(ml_dtypes.bfloat16)).reshape(k // 32, 32, n)
    amax = np.abs(w).max(1)
    if fmt == "e4m3":
        byte = np.frexp(amax)[1] - 1 + 127 - 7
    else:
        mant, ex = np.frexp(amax / 6.0)
        byte = np.where(mant > 0.5, ex, ex - 1) + 127
    byte = np.clip(np.where(amax > 0, byte, 1), 1, 254)
    scaled = (w * np.exp2(127.0 - byte)[:, None, :]).reshape(k, n).astype(np.float32)
    by_word = np.ascontiguousarray(scaled.reshape(k // 512, 128, 4, n).transpose(0, 1, 3, 2))
    if fmt == "e4m3":
        words = by_word.astype(ml_dtypes.float8_e4m3fn).view(np.uint8)
    else:
        c = by_word.astype(ml_dtypes.float4_e2m1fn).view(np.uint8) & 0xF
        words = (c[..., 0::2] | (c[..., 1::2] << 4)).reshape(k // 512, 128, 2 * n)
    return np.ascontiguousarray(words), np.ascontiguousarray(byte.astype(np.uint8).reshape(k // 512, 16, n))


def unpack_weight(words, scales, fmt):
    g, _, n = scales.shape
    words = np.ascontiguousarray(words).reshape(g, 128, n, -1)
    if fmt == "e4m3":
        vals = words.view(ml_dtypes.float8_e4m3fn).astype(np.float64)
    else:
        nib = np.empty((g, 128, n, 4), np.uint8)
        nib[..., 0::2] = words & 0xF
        nib[..., 1::2] = words >> 4
        vals = E2M1[nib]
    vals = vals * np.repeat(np.exp2(scales.astype(np.float64) - 127.0), 8, axis=1)[..., None]
    return vals.transpose(0, 1, 3, 2).reshape(g * 512, n)


def pack_table4(v):
    words, scales = pack_weight(v, "e2m1")
    g, t = words.shape[0] // 2, v.shape[1]
    return np.ascontiguousarray(words.reshape(g, 2, 128, t, 2).transpose(0, 2, 3, 1, 4).reshape(g, 128, t, 4)), scales


def unpack_table4(words, scales):
    g, _, t, _ = words.shape
    return unpack_weight(words.reshape(g, 128, t, 2, 2).transpose(0, 3, 1, 2, 4).reshape(2 * g, 128, 2 * t), scales, "e2m1")


K, N, T, J = 1024, 512, 4096, 2048


def setup_inputs():
    n = np.random.standard_normal
    s = mx_kscale(K)[:, None]
    p_tab = pack_table4(n((K, T)) * s)
    p_tab2 = pack_table4(n((K, T)) * s)
    p_wi = pack_weight(n((K, N)) / np.sqrt(2 * K) / s, "e2m1")
    return {
        "tab_words": p_tab[0],
        "tab_scales": p_tab[1],
        "tab2_words": p_tab2[0],
        "tab2_scales": p_tab2[1],
        "wr": (n((K, N)) / np.sqrt(2 * K) / s).astype(np.float32),
        "wi_words": p_wi[0],
        "wi_scales": p_wi[1],
        "offs": striped(np.random.permutation(T)[:J]),
    }


def reference(tab_words, tab_scales, tab2_words, tab2_scales, wr, wi_words, wi_scales, offs):
    idx = unstriped(offs)
    tab_ = unpack_table4(tab_words, tab_scales)[:, idx]
    tab2_ = unpack_table4(tab2_words, tab2_scales)[:, idx]
    wr_ = mxq(f64(wr), 0, "e4m3")
    wi_ = unpack_weight(wi_words, wi_scales, "e2m1")
    rr = wr_.T @ tab_
    ii = wi_.T @ tab2_
    zr = rr - ii
    ri = wr_.T @ tab2_ + wi_.T @ tab_
    zi = ri
    return np.sqrt((zr) ** 2 + (zi) ** 2)

@@ -1,0 +1,260 @@
+from contextlib import ExitStack
+
+import concourse.mybir as mybir
+
+K, N, T, J = 1024, 512, 4096, 2048
+FLOPS = 4 * 2 * K * N * J
+
+F32 = mybir.dt.float32
+BF16 = mybir.dt.bfloat16
+I32 = mybir.dt.int32
+U32 = mybir.dt.uint32
+U16 = mybir.dt.uint16
+U8 = mybir.dt.uint8
+FP8X4 = mybir.dt.float8_e4m3fn_x4
+FP4X4 = mybir.dt.float4_e2m1fn_x4
+ACT = mybir.ActivationFunctionType
+ALU = mybir.AluOpType
+
+P = 128
+PACK = 4
+PASSES = 2
+NT = N // P
+JW = 512
+JS = J // JW
+SHIFT = 16
+ROOT_LAG = 2
+VECTOR_SQUARES_FROM = 12
+
+
+def tile_list_cpxtab_mag_kernel(
+    tc, tab_words, tab_scales, tab2_words, tab2_scales, wr, wi_words, wi_scales, offs, out
+):
+    nc = tc.nc
+    with ExitStack() as ctx:
+        lists = ctx.enter_context(tc.tile_pool(name="lists", bufs=1))
+        keep = ctx.enter_context(tc.tile_pool(name="keep", bufs=1))
+        stage = ctx.enter_context(tc.tile_pool(name="stage", bufs=4))
+        tail = ctx.enter_context(tc.tile_pool(name="tail", bufs=6))
+        psum = ctx.enter_context(tc.psum_pool(name="psum", bufs=4))
+
+        offsets = lists.tile([P, J // 16], U16, name="offsets")
+        nc.sync.dma_start(offsets[:], offs)
+
+        wi_codes = keep.tile([P, PASSES, 2 * N // 4], I32, name="wi_codes", align_bytes=64)
+        nc.sync.dma_start(wi_codes[:], wi_words.bitcast(I32).rearrange("a p w -> p a w"))
+
+        word_win = [keep.tile([P, T], I32, name="word_win%d" % b, align_bytes=64) for b in range(2)]
+        for b, src in enumerate((tab_words, tab2_words)):
+            nc.sync.dma_start(word_win[b][:], src[0].rearrange("p t c -> p (t c)").bitcast(I32))
+
+        wr_raw = [keep.tile([P, PACK, N], F32, name="wr_raw%d" % a, align_bytes=64) for a in range(PASSES)]
+        for a in range(PASSES):
+            nc.sync.dma_start(
+                wr_raw[a][:], wr[a * P * PACK : (a + 1) * P * PACK, :].rearrange("(p i) n -> p i n", i=PACK)
+            )
+
+        scale_win = [keep.tile([P, T // 4], I32, name="scale_win%d" % b, align_bytes=64) for b in range(2)]
+        wi_plane = keep.tile([P, PASSES, N // 4], I32, name="wi_plane", align_bytes=64)
+        moved = [keep.tile([P, J // 4], I32, name="moved%d" % b, align_bytes=64) for b in range(2)]
+        nc.vector.memset(scale_win[1][:], 0)
+        nc.vector.memset(scale_win[0][:], 0)
+        nc.vector.memset(wi_plane[:], 0)
+        for b, (src, queue) in enumerate(((tab_scales, nc.scalar), (tab2_scales, nc.gpsimd))):
+            rows = src.bitcast(I32).rearrange("a (q r) w -> r q a w", r=4)
+            for r in range(4):
+                queue.dma_start(scale_win[b][r:P:SHIFT, :], rows[r])
+        wi_rows = wi_scales.bitcast(I32).rearrange("a (q r) w -> r q a w", r=4)
+        for r in range(4):
+            nc.gpsimd.dma_start(wi_plane[r:P:32, :, :], wi_rows[r])
+        for b in range(2):
+            nc.vector.memset(moved[b][:], 0)
+
+        warm_in = keep.tile([P, 1], F32, name="warm_in")
+        warm_out = keep.tile([P, 1], F32, name="warm_out")
+        nc.vector.memset(warm_in[:], 1.0)
+        nc.scalar.activation(warm_out[:], warm_in[:], ACT.Sqrt)
+
+        planes = {}
+        codes = {}
+
+        def list_slice(s):
+            return offsets[:, s * (JW // 16) : (s + 1) * (JW // 16)]
+
+        def fetch_scales(b, slices, tag, queue):
+            picked = keep.tile([P, len(slices) * JW // 4], I32, name="picked_scales", tag=tag, align_bytes=64)
+            for place, s in enumerate(slices):
+                planes[b, s] = picked[:].bitcast(U8)[:, place * JW : (place + 1) * JW]
+
+            def gather(s):
+                nc.vector.tensor_copy(planes[b, s], scale_win[b][:].bitcast(U8).indirect(list_slice(s)))
+                if s == slices[-1]:
+                    cols = slice(slices[0] * JW // 4, (s + 1) * JW // 4)
+                    queue.dma_start(moved[b][0 : P - SHIFT, cols], picked[SHIFT:P, :])
+
+            return gather
+
+        def gather_words(b, s, tag):
+            picked = keep.tile([P, JW], U32, name="picked_words", tag=tag, align_bytes=64)
+            nc.vector.tensor_copy(picked[:], word_win[b][:].bitcast(U32).indirect(list_slice(s)))
+            return picked
+
+        def part_words(b, s, picked):
+            codes[b, s] = keep.tile([P, PASSES, 2 * JW], U8, name="codes%d_%d" % (b, s), align_bytes=64)
+            nc.vector.tensor_copy(
+                codes[b, s][:].bitcast(U16), picked[:].bitcast(U16).rearrange("p (j d) -> p d j", d=PASSES)
+            )
+
+        def fetch_words(b, s, tag):
+            part_words(b, s, gather_words(b, s, tag))
+
+        wr_codes = keep.tile([P, PASSES, NT, 2, P], U32, name="wr_codes", align_bytes=64)
+        wr_plane = keep.tile([P, PASSES, NT, 2, P], U8, name="wr_plane", align_bytes=64)
+
+        def round_wr(a, t):
+            signed = stage.tile([P, 2, P, PACK], BF16, name="signed", align_bytes=64)
+            nc.scalar.activation(
+                signed[:, 0, :, :].rearrange("p (c e) i -> p c i e", e=4),
+                wr_raw[a][:, :, t * P : (t + 1) * P].rearrange("p i (c e) -> p c i e", e=4),
+                ACT.Copy,
+            )
+            return signed
+
+        def negate_wr(signed):
+            nc.vector.tensor_scalar(
+                out=signed[:, 1, :, :], in0=signed[:, 0, :, :], scalar1=-1.0, scalar2=None, op0=ALU.mult
+            )
+
+        def quantise_wr(a, t, sign, signed):
+            nc.vector.quantize_mx(
+                out=wr_codes[:, a, t, sign, :].bitcast(FP8X4),
+                scales=wr_plane[:, a, t, sign, :],
+                in_=signed[:, sign, :, :].rearrange("p n i -> p (n i)"),
+            )
+
+        def table_operand(b, s, a):
+            plane = planes[b, s] if a == 0 else moved[b][:].bitcast(U8)[:, s * JW : (s + 1) * JW]
+            return codes[b, s][:, a, :].bitcast(FP4X4), plane
+
+        def wi_pass(bank, t, b, s, a, start):
+            rhs, rhs_scale = table_operand(b, s, a)
+            nc.tensor.matmul_mx(
+                out=bank[:],
+                lhsT=wi_codes[:, a, :].bitcast(U8)[:, 2 * t * P : 2 * (t + 1) * P].bitcast(FP4X4),
+                lhsT_scale=wi_plane[:, a, :].bitcast(U8)[:, t * P : (t + 1) * P],
+                rhs=rhs,
+                rhs_scale=rhs_scale,
+                start=start,
+                stop=False,
+            )
+
+        def wr_pass(bank, t, sign, b, s, a, stop):
+            rhs, rhs_scale = table_operand(b, s, a)
+            nc.tensor.matmul_mx(
+                out=bank[:],
+                lhsT=wr_codes[:, a, t, sign, :].bitcast(FP8X4),
+                lhsT_scale=wr_plane[:, a, t, sign, :],
+                rhs=rhs,
+                rhs_scale=rhs_scale,
+                start=False,
+                stop=stop,
+            )
+
+        def sum_of_squares(real_bank, imag_bank, unit, pieces):
+            real_sq = keep.tile([P, JW], F32, name="real_sq", tag="real_sq%d" % unit, align_bytes=64)
+            imag_sq = tail.tile([P, JW], F32, name="imag_sq")
+            total = tail.tile([P, JW], F32, name="total")
+            if unit < VECTOR_SQUARES_FROM:
+                nc.scalar.activation(real_sq[:], real_bank[:], ACT.Square)
+            else:
+                real_part = tail.tile([P, JW], F32, name="real_part")
+                nc.vector.tensor_copy(real_part[:], real_bank[:])
+                nc.vector.tensor_tensor(real_sq[:], real_part[:], real_part[:], ALU.mult)
+            width = JW // pieces
+            for c0 in range(0, JW, width):
+                cols = slice(c0, c0 + width)
+                nc.scalar.activation(imag_sq[:, cols], imag_bank[:, cols], ACT.Square)
+                nc.vector.tensor_tensor(total[:, cols], real_sq[:, cols], imag_sq[:, cols], ALU.add)
+            if unit in fetch_after:
+                kind, b, s = fetch_after[unit]
+                if kind == "words":
+                    fetch_words(b, s, "real_sq%d" % unit)
+                else:
+                    fetch_scales(b, [s], "real_sq%d" % unit, nc.sync)(s)
+            waiting.append((total, unit, pieces))
+            if len(waiting) > ROOT_LAG:
+                root_and_store(*waiting.pop(0))
+
+        def root_and_store(total, unit, pieces):
+            s, t = divmod(unit, NT)
+            result = tail.tile([P, JW], F32, name="result")
+            width = JW // pieces
+            for c0 in range(0, JW, width):
+                cols = slice(c0, c0 + width)
+                nc.scalar.activation(result[:, cols], total[:, cols], ACT.Sqrt)
+                nc.sync.dma_start(out[t * P : (t + 1) * P, s * JW + c0 : s * JW + c0 + width], result[:, cols])
+
+        waiting = []
+        fetch_after = {
+            0: ("words", 0, 2),
+            2: ("words", 1, 2),
+            4: ("scales", 0, 3),
+            5: ("scales", 1, 3),
+            6: ("words", 0, 3),
+            8: ("words", 1, 3),
+        }
+
+        head = [fetch_scales(b, [0, 1], "head_scales%d" % b, nc.scalar) for b in range(2)]
+        head[0](0)
+        head[0](1)
+        fetch_scales(0, [2], "third_scales", nc.sync)(2)
+        head[1](0)
+        fetch_words(0, 0, "picked_words0")
+        head[1](1)
+        fetch_words(0, 1, "picked_words0")
+        fetch_words(1, 0, "picked_words1")
+        picked_next = gather_words(1, 1, "picked_words1")
+        units = [(a, t) for a in range(PASSES) for t in range(NT)]
+        previous = None
+        for a, t in units:
+            signed = round_wr(a, t)
+            quantise_wr(a, t, 0, signed)
+            if previous is not None:
+                quantise_wr(*previous)
+            negate_wr(signed)
+            previous = (a, t, 1, signed)
+        part_words(1, 1, picked_next)
+        quantise_wr(*previous)
+        fetch_scales(1, [2], "wr_raw1", nc.sync)(2)
+
+        real = [psum.tile([P, JW], F32, name="real") for t in range(NT)]
+        imag = [psum.tile([P, JW], F32, name="imag") for t in range(NT)]
+        for a in range(PASSES):
+            for t in range(NT):
+                wi_pass(imag[t], t, 0, 0, a, a == 0)
+        for a in range(PASSES):
+            for t in range(NT):
+                wi_pass(real[t], t, 1, 0, a, a == 0)
+        for a in range(PASSES):
+            for t in range(NT):
+                wr_pass(imag[t], t, 0, 1, 0, a, a == PASSES - 1)
+                wr_pass(real[t], t, 1, 0, 0, a, a == PASSES - 1)
+                if a == PASSES - 1:
+                    sum_of_squares(real[t], imag[t], t, 1)
+
+        for s in range(1, JS):
+            for t in range(NT):
+                real_bank = psum.tile([P, JW], F32, name="real")
+                imag_bank = psum.tile([P, JW], F32, name="imag")
+                for a in range(PASSES):
+                    wi_pass(real_bank, t, 1, s, a, a == 0)
+                for a in range(PASSES):
+                    wr_pass(real_bank, t, 1, 0, s, a, a == PASSES - 1)
+                for a in range(PASSES):
+                    wi_pass(imag_bank, t, 0, s, a, a == 0)
+                for a in range(PASSES):
+                    wr_pass(imag_bank, t, 0, 1, s, a, a == PASSES - 1)
+                unit = s * NT + t
+                sum_of_squares(real_bank, imag_bank, unit, 2 if unit == JS * NT - 1 else 1)
+        for left in waiting:
+            root_and_store(*left)

@@ -24,7 +24,9 @@ JW = 512
 JS = J // JW
 SHIFT = 16
 ROOT_LAG = 2
-VECTOR_SQUARES_FROM = 12
+WR_PIECES = [(0, 0, 2), (0, 2, 4), (1, 0, 2), (1, 2, 3), (1, 3, 4)]
+VECTOR_ADDS_FROM = 10
+VECTOR_SQUARES = range(10, 15)
 
 
 def tile_list_cpxtab_mag_kernel(
@@ -34,7 +36,6 @@ def tile_list_cpxtab_mag_kernel(
     with ExitStack() as ctx:
         lists = ctx.enter_context(tc.tile_pool(name="lists", bufs=1))
         keep = ctx.enter_context(tc.tile_pool(name="keep", bufs=1))
-        stage = ctx.enter_context(tc.tile_pool(name="stage", bufs=4))
         tail = ctx.enter_context(tc.tile_pool(name="tail", bufs=6))
         psum = ctx.enter_context(tc.psum_pool(name="psum", bufs=4))
 
@@ -44,31 +45,42 @@ def tile_list_cpxtab_mag_kernel(
         wi_codes = keep.tile([P, PASSES, 2 * N // 4], I32, name="wi_codes", align_bytes=64)
         nc.sync.dma_start(wi_codes[:], wi_words.bitcast(I32).rearrange("a p w -> p a w"))
 
+        scale_win = [keep.tile([P, T // 4], I32, name="scale_win%d" % b, align_bytes=64) for b in range(2)]
+        wi_plane = keep.tile([P, PASSES, N // 4], I32, name="wi_plane", align_bytes=64)
+        moved = [keep.tile([P, J // 4], I32, name="moved%d" % b, align_bytes=64) for b in range(2)]
+        for zeroed in (wi_plane, scale_win[0]):
+            nc.vector.memset(zeroed[:], 0)
+        for zeroed in (scale_win[1], moved[0], moved[1]):
+            nc.gpsimd.memset(zeroed[:], 0)
+
         word_win = [keep.tile([P, T], I32, name="word_win%d" % b, align_bytes=64) for b in range(2)]
-        for b, src in enumerate((tab_words, tab2_words)):
-            nc.sync.dma_start(word_win[b][:], src[0].rearrange("p t c -> p (t c)").bitcast(I32))
+
+        def load_wi_scales(r):
+            rows = wi_scales.bitcast(I32).rearrange("a (q r) w -> r q a w", r=4)
+            nc.sync.dma_start(wi_plane[r:P:32, :, :], rows[r])
+
+        def load_table_scales(b, scales):
+            rows = scales.bitcast(I32).rearrange("a (q r) w -> r q a w", r=4)
+            for r in range(4):
+                nc.sync.dma_start(scale_win[b][r:P:SHIFT, :], rows[r])
+
+        def load_table_words(b, words):
+            nc.sync.dma_start(word_win[b][:], words[0].rearrange("p t c -> p (t c)").bitcast(I32))
+
+        load_wi_scales(0)
+        load_wi_scales(1)
+        load_table_scales(0, tab_scales)
+        load_table_scales(1, tab2_scales)
+        load_table_words(0, tab_words)
+        load_wi_scales(2)
+        load_wi_scales(3)
+        load_table_words(1, tab2_words)
 
         wr_raw = [keep.tile([P, PACK, N], F32, name="wr_raw%d" % a, align_bytes=64) for a in range(PASSES)]
         for a in range(PASSES):
             nc.sync.dma_start(
                 wr_raw[a][:], wr[a * P * PACK : (a + 1) * P * PACK, :].rearrange("(p i) n -> p i n", i=PACK)
             )
-
-        scale_win = [keep.tile([P, T // 4], I32, name="scale_win%d" % b, align_bytes=64) for b in range(2)]
-        wi_plane = keep.tile([P, PASSES, N // 4], I32, name="wi_plane", align_bytes=64)
-        moved = [keep.tile([P, J // 4], I32, name="moved%d" % b, align_bytes=64) for b in range(2)]
-        nc.vector.memset(scale_win[1][:], 0)
-        nc.vector.memset(scale_win[0][:], 0)
-        nc.vector.memset(wi_plane[:], 0)
-        for b, (src, queue) in enumerate(((tab_scales, nc.scalar), (tab2_scales, nc.gpsimd))):
-            rows = src.bitcast(I32).rearrange("a (q r) w -> r q a w", r=4)
-            for r in range(4):
-                queue.dma_start(scale_win[b][r:P:SHIFT, :], rows[r])
-        wi_rows = wi_scales.bitcast(I32).rearrange("a (q r) w -> r q a w", r=4)
-        for r in range(4):
-            nc.gpsimd.dma_start(wi_plane[r:P:32, :, :], wi_rows[r])
-        for b in range(2):
-            nc.vector.memset(moved[b][:], 0)
 
         warm_in = keep.tile([P, 1], F32, name="warm_in")
         warm_out = keep.tile([P, 1], F32, name="warm_out")
@@ -86,11 +98,12 @@ def tile_list_cpxtab_mag_kernel(
             for place, s in enumerate(slices):
                 planes[b, s] = picked[:].bitcast(U8)[:, place * JW : (place + 1) * JW]
 
-            def gather(s):
+            def gather(s, move_from):
                 nc.vector.tensor_copy(planes[b, s], scale_win[b][:].bitcast(U8).indirect(list_slice(s)))
-                if s == slices[-1]:
-                    cols = slice(slices[0] * JW // 4, (s + 1) * JW // 4)
-                    queue.dma_start(moved[b][0 : P - SHIFT, cols], picked[SHIFT:P, :])
+                if move_from is not None:
+                    cols = slice(move_from * JW // 4, (s + 1) * JW // 4)
+                    own = slice((move_from - slices[0]) * JW // 4, (s + 1 - slices[0]) * JW // 4)
+                    queue.dma_start(moved[b][0 : P - SHIFT, cols], picked[SHIFT:P, own])
 
             return gather
 
@@ -99,23 +112,23 @@ def tile_list_cpxtab_mag_kernel(
             nc.vector.tensor_copy(picked[:], word_win[b][:].bitcast(U32).indirect(list_slice(s)))
             return picked
 
-        def part_words(b, s, picked):
-            codes[b, s] = keep.tile([P, PASSES, 2 * JW], U8, name="codes%d_%d" % (b, s), align_bytes=64)
+        def part_words(b, s, picked, tag):
+            codes[b, s] = keep.tile([P, PASSES, 2 * JW], U8, name="codes", tag=tag, align_bytes=64)
             nc.vector.tensor_copy(
                 codes[b, s][:].bitcast(U16), picked[:].bitcast(U16).rearrange("p (j d) -> p d j", d=PASSES)
             )
 
         def fetch_words(b, s, tag):
-            part_words(b, s, gather_words(b, s, tag))
+            part_words(b, s, gather_words(b, s, tag), "codes%d_%d" % (b, s))
 
-        wr_codes = keep.tile([P, PASSES, NT, 2, P], U32, name="wr_codes", align_bytes=64)
-        wr_plane = keep.tile([P, PASSES, NT, 2, P], U8, name="wr_plane", align_bytes=64)
+        wr_codes = keep.tile([P, PASSES, 2, N], U32, name="wr_codes", align_bytes=64)
+        wr_plane = keep.tile([P, PASSES, 2, N], U8, name="wr_plane", align_bytes=64)
 
-        def round_wr(a, t):
-            signed = stage.tile([P, 2, P, PACK], BF16, name="signed", align_bytes=64)
+        def round_wr(piece, a, cols):
+            signed = keep.tile([P, 2, cols.stop - cols.start, PACK], BF16, name="signed%d" % piece, align_bytes=64)
             nc.scalar.activation(
                 signed[:, 0, :, :].rearrange("p (c e) i -> p c i e", e=4),
-                wr_raw[a][:, :, t * P : (t + 1) * P].rearrange("p i (c e) -> p c i e", e=4),
+                wr_raw[a][:, :, cols].rearrange("p i (c e) -> p c i e", e=4),
                 ACT.Copy,
             )
             return signed
@@ -125,10 +138,10 @@ def tile_list_cpxtab_mag_kernel(
                 out=signed[:, 1, :, :], in0=signed[:, 0, :, :], scalar1=-1.0, scalar2=None, op0=ALU.mult
             )
 
-        def quantise_wr(a, t, sign, signed):
+        def quantise_wr(a, cols, sign, signed):
             nc.vector.quantize_mx(
-                out=wr_codes[:, a, t, sign, :].bitcast(FP8X4),
-                scales=wr_plane[:, a, t, sign, :],
+                out=wr_codes[:, a, sign, cols].bitcast(FP8X4),
+                scales=wr_plane[:, a, sign, cols],
                 in_=signed[:, sign, :, :].rearrange("p n i -> p (n i)"),
             )
 
@@ -152,8 +165,8 @@ def tile_list_cpxtab_mag_kernel(
             rhs, rhs_scale = table_operand(b, s, a)
             nc.tensor.matmul_mx(
                 out=bank[:],
-                lhsT=wr_codes[:, a, t, sign, :].bitcast(FP8X4),
-                lhsT_scale=wr_plane[:, a, t, sign, :],
+                lhsT=wr_codes[:, a, sign, t * P : (t + 1) * P].bitcast(FP8X4),
+                lhsT_scale=wr_plane[:, a, sign, t * P : (t + 1) * P],
                 rhs=rhs,
                 rhs_scale=rhs_scale,
                 start=False,
@@ -161,26 +174,23 @@ def tile_list_cpxtab_mag_kernel(
             )
 
         def sum_of_squares(real_bank, imag_bank, unit, pieces):
-            real_sq = keep.tile([P, JW], F32, name="real_sq", tag="real_sq%d" % unit, align_bytes=64)
+            real_sq = tail.tile([P, JW], F32, name="real_sq")
             imag_sq = tail.tile([P, JW], F32, name="imag_sq")
             total = tail.tile([P, JW], F32, name="total")
-            if unit < VECTOR_SQUARES_FROM:
-                nc.scalar.activation(real_sq[:], real_bank[:], ACT.Square)
-            else:
-                real_part = tail.tile([P, JW], F32, name="real_part")
-                nc.vector.tensor_copy(real_part[:], real_bank[:])
-                nc.vector.tensor_tensor(real_sq[:], real_part[:], real_part[:], ALU.mult)
+            nc.scalar.activation(real_sq[:], real_bank[:], ACT.Square)
+            while unit >= VECTOR_ADDS_FROM and waiting:
+                root_and_store(*waiting.pop(0))
+            if unit in VECTOR_SQUARES:
+                imag_part = tail.tile([P, JW], F32, name="imag_part")
+                nc.vector.tensor_copy(imag_part[:], imag_bank[:])
+                nc.vector.tensor_tensor(imag_sq[:], imag_part[:], imag_part[:], ALU.mult)
             width = JW // pieces
             for c0 in range(0, JW, width):
                 cols = slice(c0, c0 + width)
-                nc.scalar.activation(imag_sq[:, cols], imag_bank[:, cols], ACT.Square)
-                nc.vector.tensor_tensor(total[:, cols], real_sq[:, cols], imag_sq[:, cols], ALU.add)
-            if unit in fetch_after:
-                kind, b, s = fetch_after[unit]
-                if kind == "words":
-                    fetch_words(b, s, "real_sq%d" % unit)
-                else:
-                    fetch_scales(b, [s], "real_sq%d" % unit, nc.sync)(s)
+                if unit not in VECTOR_SQUARES:
+                    nc.scalar.activation(imag_sq[:, cols], imag_bank[:, cols], ACT.Square)
+                adder = nc.gpsimd if unit < VECTOR_ADDS_FROM else nc.vector
+                adder.tensor_tensor(total[:, cols], real_sq[:, cols], imag_sq[:, cols], ALU.add)
             waiting.append((total, unit, pieces))
             if len(waiting) > ROOT_LAG:
                 root_and_store(*waiting.pop(0))
@@ -195,37 +205,36 @@ def tile_list_cpxtab_mag_kernel(
                 nc.sync.dma_start(out[t * P : (t + 1) * P, s * JW + c0 : s * JW + c0 + width], result[:, cols])
 
         waiting = []
-        fetch_after = {
-            0: ("words", 0, 2),
-            2: ("words", 1, 2),
-            4: ("scales", 0, 3),
-            5: ("scales", 1, 3),
-            6: ("words", 0, 3),
-            8: ("words", 1, 3),
-        }
 
         head = [fetch_scales(b, [0, 1], "head_scales%d" % b, nc.scalar) for b in range(2)]
-        head[0](0)
-        head[0](1)
-        fetch_scales(0, [2], "third_scales", nc.sync)(2)
-        head[1](0)
+        head[0](0, None)
+        head[0](1, 0)
+        head[1](0, None)
+        head[1](1, 0)
         fetch_words(0, 0, "picked_words0")
-        head[1](1)
         fetch_words(0, 1, "picked_words0")
         fetch_words(1, 0, "picked_words1")
         picked_next = gather_words(1, 1, "picked_words1")
-        units = [(a, t) for a in range(PASSES) for t in range(NT)]
         previous = None
-        for a, t in units:
-            signed = round_wr(a, t)
-            quantise_wr(a, t, 0, signed)
+        for piece, (a, t0, t1) in enumerate(WR_PIECES):
+            cols = slice(t0 * P, t1 * P)
+            signed = round_wr(piece, a, cols)
+            quantise_wr(a, cols, 0, signed)
             if previous is not None:
                 quantise_wr(*previous)
             negate_wr(signed)
-            previous = (a, t, 1, signed)
-        part_words(1, 1, picked_next)
+            previous = (a, cols, 1, signed)
+        part_words(1, 1, picked_next, "wr_raw1")
         quantise_wr(*previous)
-        fetch_scales(1, [2], "wr_raw1", nc.sync)(2)
+        late = [fetch_scales(b, [2, 3], tag, nc.sync) for b, tag in enumerate(("signed3", "picked_words1"))]
+        late[1](2, 2)
+        late[0](2, 2)
+        fetch_words(0, 2, "signed4")
+        fetch_words(1, 2, "signed4")
+        late[1](3, 3)
+        late[0](3, 3)
+        fetch_words(0, 3, "signed4")
+        fetch_words(1, 3, "signed4")
 
         real = [psum.tile([P, JW], F32, name="real") for t in range(NT)]
         imag = [psum.tile([P, JW], F32, name="imag") for t in range(NT)]

@@ -25,8 +25,11 @@ JS = J // JW
 SHIFT = 16
 ROOT_LAG = 2
 WR_PIECES = [(0, 0, 2), (0, 2, 4), (1, 0, 2), (1, 2, 3), (1, 3, 4)]
-VECTOR_ADDS_FROM = 10
-VECTOR_SQUARES = range(10, 15)
+LAST_UNIT = JS * NT - 1
+HALVES_FROM = 8
+VECTOR_SQUARES = (8, 10, 12, 15)
+WHOLE = [slice(0, JW)]
+HALVES = [slice(0, JW // 2), slice(JW // 2, JW)]
 
 
 def tile_list_cpxtab_mag_kernel(
@@ -48,10 +51,8 @@ def tile_list_cpxtab_mag_kernel(
         scale_win = [keep.tile([P, T // 4], I32, name="scale_win%d" % b, align_bytes=64) for b in range(2)]
         wi_plane = keep.tile([P, PASSES, N // 4], I32, name="wi_plane", align_bytes=64)
         moved = [keep.tile([P, J // 4], I32, name="moved%d" % b, align_bytes=64) for b in range(2)]
-        for zeroed in (wi_plane, scale_win[0]):
+        for zeroed in (wi_plane, scale_win[0], scale_win[1], moved[0], moved[1]):
             nc.vector.memset(zeroed[:], 0)
-        for zeroed in (scale_win[1], moved[0], moved[1]):
-            nc.gpsimd.memset(zeroed[:], 0)
 
         word_win = [keep.tile([P, T], I32, name="word_win%d" % b, align_bytes=64) for b in range(2)]
 
@@ -74,13 +75,12 @@ def tile_list_cpxtab_mag_kernel(
         load_table_words(0, tab_words)
         load_wi_scales(2)
         load_wi_scales(3)
-        load_table_words(1, tab2_words)
 
         wr_raw = [keep.tile([P, PACK, N], F32, name="wr_raw%d" % a, align_bytes=64) for a in range(PASSES)]
-        for a in range(PASSES):
-            nc.sync.dma_start(
-                wr_raw[a][:], wr[a * P * PACK : (a + 1) * P * PACK, :].rearrange("(p i) n -> p i n", i=PACK)
-            )
+
+        def load_wr(a):
+            rows = wr[a * P * PACK : (a + 1) * P * PACK, :]
+            nc.sync.dma_start(wr_raw[a][:], rows.rearrange("(p i) n -> p i n", i=PACK))
 
         warm_in = keep.tile([P, 1], F32, name="warm_in")
         warm_out = keep.tile([P, 1], F32, name="warm_out")
@@ -93,7 +93,7 @@ def tile_list_cpxtab_mag_kernel(
         def list_slice(s):
             return offsets[:, s * (JW // 16) : (s + 1) * (JW // 16)]
 
-        def fetch_scales(b, slices, tag, queue):
+        def fetch_scales(b, slices, tag):
             picked = keep.tile([P, len(slices) * JW // 4], I32, name="picked_scales", tag=tag, align_bytes=64)
             for place, s in enumerate(slices):
                 planes[b, s] = picked[:].bitcast(U8)[:, place * JW : (place + 1) * JW]
@@ -103,23 +103,23 @@ def tile_list_cpxtab_mag_kernel(
                 if move_from is not None:
                     cols = slice(move_from * JW // 4, (s + 1) * JW // 4)
                     own = slice((move_from - slices[0]) * JW // 4, (s + 1 - slices[0]) * JW // 4)
-                    queue.dma_start(moved[b][0 : P - SHIFT, cols], picked[SHIFT:P, own])
+                    nc.sync.dma_start(moved[b][0 : P - SHIFT, cols], picked[SHIFT:P, own])
 
             return gather
 
-        def gather_words(b, s, tag):
-            picked = keep.tile([P, JW], U32, name="picked_words", tag=tag, align_bytes=64)
-            nc.vector.tensor_copy(picked[:], word_win[b][:].bitcast(U32).indirect(list_slice(s)))
-            return picked
+        def gather_words(b, s, picked):
+            nc.vector.tensor_copy(picked, word_win[b][:].bitcast(U32).indirect(list_slice(s)))
 
         def part_words(b, s, picked, tag):
             codes[b, s] = keep.tile([P, PASSES, 2 * JW], U8, name="codes", tag=tag, align_bytes=64)
             nc.vector.tensor_copy(
-                codes[b, s][:].bitcast(U16), picked[:].bitcast(U16).rearrange("p (j d) -> p d j", d=PASSES)
+                codes[b, s][:].bitcast(U16), picked.bitcast(U16).rearrange("p (j d) -> p d j", d=PASSES)
             )
 
         def fetch_words(b, s, tag):
-            part_words(b, s, gather_words(b, s, tag), "codes%d_%d" % (b, s))
+            picked = keep.tile([P, JW], U32, name="picked_words", tag=tag, align_bytes=64)
+            gather_words(b, s, picked[:])
+            part_words(b, s, picked[:], "codes%d_%d" % (b, s))
 
         wr_codes = keep.tile([P, PASSES, 2, N], U32, name="wr_codes", align_bytes=64)
         wr_plane = keep.tile([P, PASSES, 2, N], U8, name="wr_plane", align_bytes=64)
@@ -173,48 +173,53 @@ def tile_list_cpxtab_mag_kernel(
                 stop=stop,
             )
 
-        def sum_of_squares(real_bank, imag_bank, unit, pieces):
+        def sum_of_squares(real_bank, imag_bank, unit):
             real_sq = tail.tile([P, JW], F32, name="real_sq")
             imag_sq = tail.tile([P, JW], F32, name="imag_sq")
             total = tail.tile([P, JW], F32, name="total")
-            nc.scalar.activation(real_sq[:], real_bank[:], ACT.Square)
-            while unit >= VECTOR_ADDS_FROM and waiting:
-                root_and_store(*waiting.pop(0))
             if unit in VECTOR_SQUARES:
-                imag_part = tail.tile([P, JW], F32, name="imag_part")
-                nc.vector.tensor_copy(imag_part[:], imag_bank[:])
-                nc.vector.tensor_tensor(imag_sq[:], imag_part[:], imag_part[:], ALU.mult)
-            width = JW // pieces
-            for c0 in range(0, JW, width):
-                cols = slice(c0, c0 + width)
-                if unit not in VECTOR_SQUARES:
-                    nc.scalar.activation(imag_sq[:, cols], imag_bank[:, cols], ACT.Square)
-                adder = nc.gpsimd if unit < VECTOR_ADDS_FROM else nc.vector
+                real_part = tail.tile([P, JW], F32, name="real_part")
+                nc.vector.tensor_copy(real_part[:], real_bank[:])
+                nc.vector.tensor_tensor(real_sq[:], real_bank[:], real_part[:], ALU.mult)
+            else:
+                nc.scalar.activation(real_sq[:], real_bank[:], ACT.Square)
+            while unit >= HALVES_FROM and len(waiting) > (1 if unit == HALVES_FROM else 0):
+                root_and_store(*waiting.pop(0))
+            for cols in HALVES if unit == LAST_UNIT else WHOLE:
+                nc.scalar.activation(imag_sq[:, cols], imag_bank[:, cols], ACT.Square)
+            for cols in HALVES if unit >= HALVES_FROM else WHOLE:
+                adder = nc.vector if unit >= HALVES_FROM else nc.gpsimd
                 adder.tensor_tensor(total[:, cols], real_sq[:, cols], imag_sq[:, cols], ALU.add)
-            waiting.append((total, unit, pieces))
+            waiting.append((total, unit))
             if len(waiting) > ROOT_LAG:
                 root_and_store(*waiting.pop(0))
 
-        def root_and_store(total, unit, pieces):
+        def root_and_store(total, unit):
             s, t = divmod(unit, NT)
             result = tail.tile([P, JW], F32, name="result")
-            width = JW // pieces
-            for c0 in range(0, JW, width):
-                cols = slice(c0, c0 + width)
+            target = out[t * P : (t + 1) * P, s * JW : (s + 1) * JW]
+            for cols in HALVES if unit >= HALVES_FROM else WHOLE:
                 nc.scalar.activation(result[:, cols], total[:, cols], ACT.Sqrt)
-                nc.sync.dma_start(out[t * P : (t + 1) * P, s * JW + c0 : s * JW + c0 + width], result[:, cols])
+                if unit == LAST_UNIT:
+                    nc.sync.dma_start(target[:, cols], result[:, cols])
+            if unit != LAST_UNIT:
+                nc.sync.dma_start(target, result[:])
 
         waiting = []
 
-        head = [fetch_scales(b, [0, 1], "head_scales%d" % b, nc.scalar) for b in range(2)]
+        head = [fetch_scales(b, [0, 1], "head_scales%d" % b) for b in range(2)]
         head[0](0, None)
         head[0](1, 0)
+        load_table_words(1, tab2_words)
         head[1](0, None)
         head[1](1, 0)
+        for a in range(PASSES):
+            load_wr(a)
         fetch_words(0, 0, "picked_words0")
         fetch_words(0, 1, "picked_words0")
         fetch_words(1, 0, "picked_words1")
-        picked_next = gather_words(1, 1, "picked_words1")
+        picked_next = keep.tile([P, JW], U32, name="picked_words", tag="picked_words1", align_bytes=64)
+        gather_words(1, 1, picked_next[:])
         previous = None
         for piece, (a, t0, t1) in enumerate(WR_PIECES):
             cols = slice(t0 * P, t1 * P)
@@ -224,17 +229,17 @@ def tile_list_cpxtab_mag_kernel(
                 quantise_wr(*previous)
             negate_wr(signed)
             previous = (a, cols, 1, signed)
-        part_words(1, 1, picked_next, "wr_raw1")
+        part_words(1, 1, picked_next[:], "wr_raw1")
         quantise_wr(*previous)
-        late = [fetch_scales(b, [2, 3], tag, nc.sync) for b, tag in enumerate(("signed3", "picked_words1"))]
-        late[1](2, 2)
-        late[0](2, 2)
-        fetch_words(0, 2, "signed4")
-        fetch_words(1, 2, "signed4")
-        late[1](3, 3)
-        late[0](3, 3)
-        fetch_words(0, 3, "signed4")
-        fetch_words(1, 3, "signed4")
+        late = [fetch_scales(b, [2, 3], tag) for b, tag in enumerate(("signed4", "picked_words1"))]
+        for s in (2, 3):
+            late[1](s, s)
+            late[0](s, s)
+            picked_both = keep.tile([P, 2, JW], U32, name="picked_both", tag="signed3", align_bytes=64)
+            for b in range(2):
+                gather_words(b, s, picked_both[:, b, :])
+            for b in range(2):
+                part_words(b, s, picked_both[:, b, :], "codes%d_%d" % (b, s))
 
         real = [psum.tile([P, JW], F32, name="real") for t in range(NT)]
         imag = [psum.tile([P, JW], F32, name="imag") for t in range(NT)]
@@ -249,7 +254,7 @@ def tile_list_cpxtab_mag_kernel(
                 wr_pass(imag[t], t, 0, 1, 0, a, a == PASSES - 1)
                 wr_pass(real[t], t, 1, 0, 0, a, a == PASSES - 1)
                 if a == PASSES - 1:
-                    sum_of_squares(real[t], imag[t], t, 1)
+                    sum_of_squares(real[t], imag[t], t)
 
         for s in range(1, JS):
             for t in range(NT):
@@ -263,7 +268,6 @@ def tile_list_cpxtab_mag_kernel(
                     wi_pass(imag_bank, t, 0, s, a, a == 0)
                 for a in range(PASSES):
                     wr_pass(imag_bank, t, 0, 1, s, a, a == PASSES - 1)
-                unit = s * NT + t
-                sum_of_squares(real_bank, imag_bank, unit, 2 if unit == JS * NT - 1 else 1)
+                sum_of_squares(real_bank, imag_bank, s * NT + t)
         for left in waiting:
             root_and_store(*left)

@@ -23,11 +23,13 @@ NT = N // P
 JW = 512
 JS = J // JW
 SHIFT = 16
-ROOT_LAG = 2
+ROOT_LAG = 4
 WR_PIECES = [(0, 0, 2), (0, 2, 4), (1, 0, 2), (1, 2, 3), (1, 3, 4)]
 LAST_UNIT = JS * NT - 1
-HALVES_FROM = 8
-VECTOR_SQUARES = (8, 10, 12, 15)
+HALVES_FROM = 14
+CATCH_UP_FROM = 8
+VECTOR_SQUARES = range(8, 15)
+GPSIMD_ADDS = range(7, 14)
 WHOLE = [slice(0, JW)]
 HALVES = [slice(0, JW // 2), slice(JW // 2, JW)]
 
@@ -39,7 +41,7 @@ def tile_list_cpxtab_mag_kernel(
     with ExitStack() as ctx:
         lists = ctx.enter_context(tc.tile_pool(name="lists", bufs=1))
         keep = ctx.enter_context(tc.tile_pool(name="keep", bufs=1))
-        tail = ctx.enter_context(tc.tile_pool(name="tail", bufs=6))
+        tail = ctx.enter_context(tc.tile_pool(name="tail", bufs=8))
         psum = ctx.enter_context(tc.psum_pool(name="psum", bufs=4))
 
         offsets = lists.tile([P, J // 16], U16, name="offsets")
@@ -121,6 +123,17 @@ def tile_list_cpxtab_mag_kernel(
             gather_words(b, s, picked[:])
             part_words(b, s, picked[:], "codes%d_%d" % (b, s))
 
+        picked_both = {}
+
+        def gather_both(s, tag):
+            picked_both[s] = keep.tile([P, 2, JW], U32, name="picked_both", tag=tag, align_bytes=64)
+            for b in range(2):
+                gather_words(b, s, picked_both[s][:, b, :])
+
+        def part_both(s):
+            for b in range(2):
+                part_words(b, s, picked_both[s][:, b, :], "codes%d_%d" % (b, s))
+
         wr_codes = keep.tile([P, PASSES, 2, N], U32, name="wr_codes", align_bytes=64)
         wr_plane = keep.tile([P, PASSES, 2, N], U8, name="wr_plane", align_bytes=64)
 
@@ -174,22 +187,30 @@ def tile_list_cpxtab_mag_kernel(
             )
 
         def sum_of_squares(real_bank, imag_bank, unit):
-            real_sq = tail.tile([P, JW], F32, name="real_sq")
+            real_sq = keep.tile([P, JW], F32, name="real_sq", tag="real_sq%d" % unit, align_bytes=64)
             imag_sq = tail.tile([P, JW], F32, name="imag_sq")
             total = tail.tile([P, JW], F32, name="total")
-            if unit in VECTOR_SQUARES:
-                real_part = tail.tile([P, JW], F32, name="real_part")
-                nc.vector.tensor_copy(real_part[:], real_bank[:])
-                nc.vector.tensor_tensor(real_sq[:], real_bank[:], real_part[:], ALU.mult)
-            else:
-                nc.scalar.activation(real_sq[:], real_bank[:], ACT.Square)
-            while unit >= HALVES_FROM and len(waiting) > (1 if unit == HALVES_FROM else 0):
+            nc.scalar.activation(real_sq[:], real_bank[:], ACT.Square)
+            while unit >= CATCH_UP_FROM and len(waiting) > max(0, ROOT_LAG - 1 - (unit - CATCH_UP_FROM)):
                 root_and_store(*waiting.pop(0))
-            for cols in HALVES if unit == LAST_UNIT else WHOLE:
-                nc.scalar.activation(imag_sq[:, cols], imag_bank[:, cols], ACT.Square)
+            if unit in VECTOR_SQUARES:
+                imag_part = tail.tile([P, JW], F32, name="imag_part")
+                nc.vector.tensor_copy(imag_part[:], imag_bank[:])
+                nc.vector.tensor_tensor(imag_sq[:], imag_bank[:], imag_part[:], ALU.mult)
+            else:
+                for cols in HALVES if unit == LAST_UNIT else WHOLE:
+                    nc.scalar.activation(imag_sq[:, cols], imag_bank[:, cols], ACT.Square)
+            adder = nc.gpsimd if unit in GPSIMD_ADDS else nc.vector
             for cols in HALVES if unit >= HALVES_FROM else WHOLE:
-                adder = nc.vector if unit >= HALVES_FROM else nc.gpsimd
                 adder.tensor_tensor(total[:, cols], real_sq[:, cols], imag_sq[:, cols], ALU.add)
+            if unit == 0:
+                part_both(2)
+            if unit in (2, 3):
+                fetch_scales(3 - unit, [3], "real_sq%d" % unit)(3, 3)
+            if unit == 4:
+                gather_both(3, "real_sq4")
+            if unit == 5:
+                part_both(3)
             waiting.append((total, unit))
             if len(waiting) > ROOT_LAG:
                 root_and_store(*waiting.pop(0))
@@ -231,15 +252,9 @@ def tile_list_cpxtab_mag_kernel(
             previous = (a, cols, 1, signed)
         part_words(1, 1, picked_next[:], "wr_raw1")
         quantise_wr(*previous)
-        late = [fetch_scales(b, [2, 3], tag) for b, tag in enumerate(("signed4", "picked_words1"))]
-        for s in (2, 3):
-            late[1](s, s)
-            late[0](s, s)
-            picked_both = keep.tile([P, 2, JW], U32, name="picked_both", tag="signed3", align_bytes=64)
-            for b in range(2):
-                gather_words(b, s, picked_both[:, b, :])
-            for b in range(2):
-                part_words(b, s, picked_both[:, b, :], "codes%d_%d" % (b, s))
+        fetch_scales(1, [2], "picked_words1")(2, 2)
+        fetch_scales(0, [2], "signed4")(2, 2)
+        gather_both(2, "signed3")
 
         real = [psum.tile([P, JW], F32, name="real") for t in range(NT)]
         imag = [psum.tile([P, JW], F32, name="imag") for t in range(NT)]

from contextlib import ExitStack

import concourse.mybir as mybir

K, N, T, J = 1024, 512, 4096, 2048
FLOPS = 4 * 2 * K * N * J

F32 = mybir.dt.float32
BF16 = mybir.dt.bfloat16
I32 = mybir.dt.int32
U32 = mybir.dt.uint32
U16 = mybir.dt.uint16
U8 = mybir.dt.uint8
FP8X4 = mybir.dt.float8_e4m3fn_x4
FP4X4 = mybir.dt.float4_e2m1fn_x4
ACT = mybir.ActivationFunctionType
ALU = mybir.AluOpType

P = 128
PACK = 4
PASSES = 2
NT = N // P
JW = 512
JS = J // JW
SHIFT = 16
ROOT_LAG = 4
WR_PIECES = [(0, 0, 2), (0, 2, 4), (1, 0, 2), (1, 2, 3), (1, 3, 4)]
LAST_UNIT = JS * NT - 1
HALVES_FROM = 14
CATCH_UP_FROM = 8
VECTOR_SQUARES = range(8, 15)
GPSIMD_ADDS = range(7, 14)
WHOLE = [slice(0, JW)]
HALVES = [slice(0, JW // 2), slice(JW // 2, JW)]


def tile_list_cpxtab_mag_kernel(
    tc, tab_words, tab_scales, tab2_words, tab2_scales, wr, wi_words, wi_scales, offs, out
):
    nc = tc.nc
    with ExitStack() as ctx:
        lists = ctx.enter_context(tc.tile_pool(name="lists", bufs=1))
        keep = ctx.enter_context(tc.tile_pool(name="keep", bufs=1))
        tail = ctx.enter_context(tc.tile_pool(name="tail", bufs=8))
        psum = ctx.enter_context(tc.psum_pool(name="psum", bufs=4))

        offsets = lists.tile([P, J // 16], U16, name="offsets")
        nc.sync.dma_start(offsets[:], offs)

        wi_codes = keep.tile([P, PASSES, 2 * N // 4], I32, name="wi_codes", align_bytes=64)
        nc.sync.dma_start(wi_codes[:], wi_words.bitcast(I32).rearrange("a p w -> p a w"))

        scale_win = [keep.tile([P, T // 4], I32, name="scale_win%d" % b, align_bytes=64) for b in range(2)]
        wi_plane = keep.tile([P, PASSES, N // 4], I32, name="wi_plane", align_bytes=64)
        moved = [keep.tile([P, J // 4], I32, name="moved%d" % b, align_bytes=64) for b in range(2)]
        for zeroed in (wi_plane, scale_win[0], scale_win[1], moved[0], moved[1]):
            nc.vector.memset(zeroed[:], 0)

        word_win = [keep.tile([P, T], I32, name="word_win%d" % b, align_bytes=64) for b in range(2)]

        def load_wi_scales(r):
            rows = wi_scales.bitcast(I32).rearrange("a (q r) w -> r q a w", r=4)
            nc.sync.dma_start(wi_plane[r:P:32, :, :], rows[r])

        def load_table_scales(b, scales):
            rows = scales.bitcast(I32).rearrange("a (q r) w -> r q a w", r=4)
            for r in range(4):
                nc.sync.dma_start(scale_win[b][r:P:SHIFT, :], rows[r])

        def load_table_words(b, words):
            nc.sync.dma_start(word_win[b][:], words[0].rearrange("p t c -> p (t c)").bitcast(I32))

        load_wi_scales(0)
        load_wi_scales(1)
        load_table_scales(0, tab_scales)
        load_table_scales(1, tab2_scales)
        load_table_words(0, tab_words)
        load_wi_scales(2)
        load_wi_scales(3)

        wr_raw = [keep.tile([P, PACK, N], F32, name="wr_raw%d" % a, align_bytes=64) for a in range(PASSES)]

        def load_wr(a):
            rows = wr[a * P * PACK : (a + 1) * P * PACK, :]
            nc.sync.dma_start(wr_raw[a][:], rows.rearrange("(p i) n -> p i n", i=PACK))

        warm_in = keep.tile([P, 1], F32, name="warm_in")
        warm_out = keep.tile([P, 1], F32, name="warm_out")
        nc.vector.memset(warm_in[:], 1.0)
        nc.scalar.activation(warm_out[:], warm_in[:], ACT.Sqrt)

        planes = {}
        codes = {}

        def list_slice(s):
            return offsets[:, s * (JW // 16) : (s + 1) * (JW // 16)]

        def fetch_scales(b, slices, tag):
            picked = keep.tile([P, len(slices) * JW // 4], I32, name="picked_scales", tag=tag, align_bytes=64)
            for place, s in enumerate(slices):
                planes[b, s] = picked[:].bitcast(U8)[:, place * JW : (place + 1) * JW]

            def gather(s, move_from):
                nc.vector.tensor_copy(planes[b, s], scale_win[b][:].bitcast(U8).indirect(list_slice(s)))
                if move_from is not None:
                    cols = slice(move_from * JW // 4, (s + 1) * JW // 4)
                    own = slice((move_from - slices[0]) * JW // 4, (s + 1 - slices[0]) * JW // 4)
                    nc.sync.dma_start(moved[b][0 : P - SHIFT, cols], picked[SHIFT:P, own])

            return gather

        def gather_words(b, s, picked):
            nc.vector.tensor_copy(picked, word_win[b][:].bitcast(U32).indirect(list_slice(s)))

        def part_words(b, s, picked, tag):
            codes[b, s] = keep.tile([P, PASSES, 2 * JW], U8, name="codes", tag=tag, align_bytes=64)
            nc.vector.tensor_copy(
                codes[b, s][:].bitcast(U16), picked.bitcast(U16).rearrange("p (j d) -> p d j", d=PASSES)
            )

        def fetch_words(b, s, tag):
            picked = keep.tile([P, JW], U32, name="picked_words", tag=tag, align_bytes=64)
            gather_words(b, s, picked[:])
            part_words(b, s, picked[:], "codes%d_%d" % (b, s))

        picked_both = {}

        def gather_both(s, tag):
            picked_both[s] = keep.tile([P, 2, JW], U32, name="picked_both", tag=tag, align_bytes=64)
            for b in range(2):
                gather_words(b, s, picked_both[s][:, b, :])

        def part_both(s):
            for b in range(2):
                part_words(b, s, picked_both[s][:, b, :], "codes%d_%d" % (b, s))

        wr_codes = keep.tile([P, PASSES, 2, N], U32, name="wr_codes", align_bytes=64)
        wr_plane = keep.tile([P, PASSES, 2, N], U8, name="wr_plane", align_bytes=64)

        def round_wr(piece, a, cols):
            signed = keep.tile([P, 2, cols.stop - cols.start, PACK], BF16, name="signed%d" % piece, align_bytes=64)
            nc.scalar.activation(
                signed[:, 0, :, :].rearrange("p (c e) i -> p c i e", e=4),
                wr_raw[a][:, :, cols].rearrange("p i (c e) -> p c i e", e=4),
                ACT.Copy,
            )
            return signed

        def negate_wr(signed):
            nc.vector.tensor_scalar(
                out=signed[:, 1, :, :], in0=signed[:, 0, :, :], scalar1=-1.0, scalar2=None, op0=ALU.mult
            )

        def quantise_wr(a, cols, sign, signed):
            nc.vector.quantize_mx(
                out=wr_codes[:, a, sign, cols].bitcast(FP8X4),
                scales=wr_plane[:, a, sign, cols],
                in_=signed[:, sign, :, :].rearrange("p n i -> p (n i)"),
            )

        def table_operand(b, s, a):
            plane = planes[b, s] if a == 0 else moved[b][:].bitcast(U8)[:, s * JW : (s + 1) * JW]
            return codes[b, s][:, a, :].bitcast(FP4X4), plane

        def wi_pass(bank, t, b, s, a, start):
            rhs, rhs_scale = table_operand(b, s, a)
            nc.tensor.matmul_mx(
                out=bank[:],
                lhsT=wi_codes[:, a, :].bitcast(U8)[:, 2 * t * P : 2 * (t + 1) * P].bitcast(FP4X4),
                lhsT_scale=wi_plane[:, a, :].bitcast(U8)[:, t * P : (t + 1) * P],
                rhs=rhs,
                rhs_scale=rhs_scale,
                start=start,
                stop=False,
            )

        def wr_pass(bank, t, sign, b, s, a, stop):
            rhs, rhs_scale = table_operand(b, s, a)
            nc.tensor.matmul_mx(
                out=bank[:],
                lhsT=wr_codes[:, a, sign, t * P : (t + 1) * P].bitcast(FP8X4),
                lhsT_scale=wr_plane[:, a, sign, t * P : (t + 1) * P],
                rhs=rhs,
                rhs_scale=rhs_scale,
                start=False,
                stop=stop,
            )

        def sum_of_squares(real_bank, imag_bank, unit):
            real_sq = keep.tile([P, JW], F32, name="real_sq", tag="real_sq%d" % unit, align_bytes=64)
            imag_sq = tail.tile([P, JW], F32, name="imag_sq")
            total = tail.tile([P, JW], F32, name="total")
            nc.scalar.activation(real_sq[:], real_bank[:], ACT.Square)
            while unit >= CATCH_UP_FROM and len(waiting) > max(0, ROOT_LAG - 1 - (unit - CATCH_UP_FROM)):
                root_and_store(*waiting.pop(0))
            if unit in VECTOR_SQUARES:
                imag_part = tail.tile([P, JW], F32, name="imag_part")
                nc.vector.tensor_copy(imag_part[:], imag_bank[:])
                nc.vector.tensor_tensor(imag_sq[:], imag_bank[:], imag_part[:], ALU.mult)
            else:
                for cols in HALVES if unit == LAST_UNIT else WHOLE:
                    nc.scalar.activation(imag_sq[:, cols], imag_bank[:, cols], ACT.Square)
            adder = nc.gpsimd if unit in GPSIMD_ADDS else nc.vector
            for cols in HALVES if unit >= HALVES_FROM else WHOLE:
                adder.tensor_tensor(total[:, cols], real_sq[:, cols], imag_sq[:, cols], ALU.add)
            if unit == 0:
                part_both(2)
            if unit in (2, 3):
                fetch_scales(3 - unit, [3], "real_sq%d" % unit)(3, 3)
            if unit == 4:
                gather_both(3, "real_sq4")
            if unit == 5:
                part_both(3)
            waiting.append((total, unit))
            if len(waiting) > ROOT_LAG:
                root_and_store(*waiting.pop(0))

        def root_and_store(total, unit):
            s, t = divmod(unit, NT)
            result = tail.tile([P, JW], F32, name="result")
            target = out[t * P : (t + 1) * P, s * JW : (s + 1) * JW]
            for cols in HALVES if unit >= HALVES_FROM else WHOLE:
                nc.scalar.activation(result[:, cols], total[:, cols], ACT.Sqrt)
                if unit == LAST_UNIT:
                    nc.sync.dma_start(target[:, cols], result[:, cols])
            if unit != LAST_UNIT:
                nc.sync.dma_start(target, result[:])

        waiting = []

        head = [fetch_scales(b, [0, 1], "head_scales%d" % b) for b in range(2)]
        head[0](0, None)
        head[0](1, 0)
        load_table_words(1, tab2_words)
        head[1](0, None)
        head[1](1, 0)
        for a in range(PASSES):
            load_wr(a)
        fetch_words(0, 0, "picked_words0")
        fetch_words(0, 1, "picked_words0")
        fetch_words(1, 0, "picked_words1")
        picked_next = keep.tile([P, JW], U32, name="picked_words", tag="picked_words1", align_bytes=64)
        gather_words(1, 1, picked_next[:])
        previous = None
        for piece, (a, t0, t1) in enumerate(WR_PIECES):
            cols = slice(t0 * P, t1 * P)
            signed = round_wr(piece, a, cols)
            quantise_wr(a, cols, 0, signed)
            if previous is not None:
                quantise_wr(*previous)
            negate_wr(signed)
            previous = (a, cols, 1, signed)
        part_words(1, 1, picked_next[:], "wr_raw1")
        quantise_wr(*previous)
        fetch_scales(1, [2], "picked_words1")(2, 2)
        fetch_scales(0, [2], "signed4")(2, 2)
        gather_both(2, "signed3")

        real = [psum.tile([P, JW], F32, name="real") for t in range(NT)]
        imag = [psum.tile([P, JW], F32, name="imag") for t in range(NT)]
        for a in range(PASSES):
            for t in range(NT):
                wi_pass(imag[t], t, 0, 0, a, a == 0)
        for a in range(PASSES):
            for t in range(NT):
                wi_pass(real[t], t, 1, 0, a, a == 0)
        for a in range(PASSES):
            for t in range(NT):
                wr_pass(imag[t], t, 0, 1, 0, a, a == PASSES - 1)
                wr_pass(real[t], t, 1, 0, 0, a, a == PASSES - 1)
                if a == PASSES - 1:
                    sum_of_squares(real[t], imag[t], t)

        for s in range(1, JS):
            for t in range(NT):
                real_bank = psum.tile([P, JW], F32, name="real")
                imag_bank = psum.tile([P, JW], F32, name="imag")
                for a in range(PASSES):
                    wi_pass(real_bank, t, 1, s, a, a == 0)
                for a in range(PASSES):
                    wr_pass(real_bank, t, 1, 0, s, a, a == PASSES - 1)
                for a in range(PASSES):
                    wi_pass(imag_bank, t, 0, s, a, a == 0)
                for a in range(PASSES):
                    wr_pass(imag_bank, t, 0, 1, s, a, a == PASSES - 1)
                sum_of_squares(real_bank, imag_bank, s * NT + t)
        for left in waiting:
            root_and_store(*left)
